import numpy as np
import ml_dtypes

BF16 = ml_dtypes.bfloat16


def bf(x):
    return np.asarray(x, np.float32).astype(BF16)


def f32(x):
    return np.asarray(x, np.float32)


def f64(x):
    return np.asarray(x).astype(np.float64)


def striped(idx):
    return np.concatenate([l.reshape(-1, 16).T for l in idx])


def rows(idx, k):
    return np.tile(np.repeat(idx, 16, axis=0), (k // (16 * 8), 1))


def look(tab, idx):
    return np.take_along_axis(f64(tab), rows(idx, len(tab)), axis=1)


K, S, V, N, M = 512, 2048, 1024, 1024, 128


def setup_inputs():
    return {"tab": f32(np.random.standard_normal((2, K, S))), "y": f32(np.random.standard_normal((K, V))), "w": bf(np.random.standard_normal((K, M)) / np.sqrt(K)), "b": f32(0.5 * np.random.standard_normal((M, 1))), "offs": striped(np.stack([np.random.permutation(S)[:N] for _ in range(8)]))}


def reference(tab, y, w, b, offs):
    idx = np.stack([g.T.reshape(-1) for g in np.split(offs, 8)])
    x = (np.minimum(look(tab[0], idx), f64(y))) * (np.tanh(look(tab[1], idx)))
    return np.maximum(f64(w).T @ x + f64(b), 0.0)

@@ -1,0 +1,55 @@
+import concourse.mybir as mybir
+
+P = 128
+PIECE = 512
+GROUP = 16
+
+FLOPS = 2 * 512 * 128 * 1024
+
+BF16, F32, U16 = mybir.dt.bfloat16, mybir.dt.float32, mybir.dt.uint16
+ALU = mybir.AluOpType
+ACT = mybir.ActivationFunctionType
+
+
+def tile_lookup_vg_mintanh_relu_kernel(tc, tab, y, w, b, offs, out):
+    nc = tc.nc
+    rows, places = tab.shape[1], tab.shape[2]
+    entries, features = y.shape[1], w.shape[1]
+    blocks, pieces = rows // P, entries // PIECE
+
+    with (
+        tc.tile_pool(name="held", bufs=1) as held,
+        tc.tile_pool(name="work", bufs=3) as work,
+        tc.psum_pool(name="psum", bufs=1) as psum,
+    ):
+        offsets = held.tile([P, entries // GROUP], U16, name="offsets")
+        nc.sync.dma_start(offsets[:], offs)
+        weights = held.tile([P, blocks, features], BF16, name="weights")
+        nc.scalar.dma_start(weights[:], w.rearrange("(k p) m -> p k m", p=P))
+        bias = held.tile([P, 1], F32, name="bias")
+        nc.scalar.dma_start(bias[:], b)
+
+        sums = [psum.tile([P, PIECE], F32, name=f"sums{c}") for c in range(pieces)]
+
+        for k in range(blocks):
+            block = slice(k * P, (k + 1) * P)
+            gates = held.tile([P, places], F32, name=f"gates{k}")
+            nc.sync.dma_start(gates[:], tab[1, block, :])
+            values = held.tile([P, places], F32, name=f"values{k}")
+            nc.sync.dma_start(values[:], tab[0, block, :])
+            stream = held.tile([P, entries], F32, name=f"stream{k}")
+            nc.sync.dma_start(stream[:], y[block, :])
+            for c in range(pieces):
+                piece = offsets[:, c * PIECE // GROUP : (c + 1) * PIECE // GROUP]
+                gate = work.tile([P, PIECE], F32, name="gate")
+                nc.scalar.activation(gate[:], gates[:].indirect(piece), ACT.Tanh)
+                least = work.tile([P, PIECE], F32, name="least")
+                nc.vector.tensor_tensor(least[:], values[:].indirect(piece), stream[:, c * PIECE : (c + 1) * PIECE], ALU.min)
+                x = work.tile([P, PIECE], BF16, name="x")
+                nc.vector.tensor_tensor(x[:], least[:], gate[:], ALU.mult)
+                nc.tensor.matmul(sums[c][:], weights[:, k, :], x[:], start=(k == 0), stop=(k == blocks - 1))
+
+        for c in range(pieces):
+            result = work.tile([P, PIECE], F32, name="result")
+            nc.scalar.activation(result[:], sums[c][:], ACT.Relu, bias=bias[:])
+            nc.sync.dma_start(out[:, c * PIECE : (c + 1) * PIECE], result[:])

@@ -1,8 +1,9 @@
 import concourse.mybir as mybir
 
 P = 128
-PIECE = 512
 GROUP = 16
+PIECE = 512
+PART = 256
 
 FLOPS = 2 * 512 * 128 * 1024
 
@@ -15,41 +16,53 @@ def tile_lookup_vg_mintanh_relu_kernel(tc, tab, y, w, b, offs, out):
     nc = tc.nc
     rows, places = tab.shape[1], tab.shape[2]
     entries, features = y.shape[1], w.shape[1]
-    blocks, pieces = rows // P, entries // PIECE
+    blocks, pieces, parts = rows // P, entries // PIECE, entries // PART
 
     with (
         tc.tile_pool(name="held", bufs=1) as held,
-        tc.tile_pool(name="work", bufs=3) as work,
+        tc.tile_pool(name="work", bufs=2) as work,
         tc.psum_pool(name="psum", bufs=1) as psum,
     ):
         offsets = held.tile([P, entries // GROUP], U16, name="offsets")
-        nc.sync.dma_start(offsets[:], offs)
         weights = held.tile([P, blocks, features], BF16, name="weights")
-        nc.scalar.dma_start(weights[:], w.rearrange("(k p) m -> p k m", p=P))
         bias = held.tile([P, 1], F32, name="bias")
-        nc.scalar.dma_start(bias[:], b)
+        values = [held.tile([P, places], F32, name=f"values{k}") for k in range(blocks)]
+        gates = [held.tile([P, places], F32, name=f"gates{k}") for k in range(blocks)]
+        streams = [held.tile([P, entries], F32, name=f"stream{k}") for k in range(blocks)]
+        sums = [psum.tile([P, PART], F32, name=f"sums{q}") for q in range(parts)]
 
-        sums = [psum.tile([P, PIECE], F32, name=f"sums{c}") for c in range(pieces)]
+        nc.scalar.dma_start(bias[:], b)
+        nc.sync.dma_start(offsets[:], offs)
+        for k in range(blocks - 1):
+            block = slice(k * P, (k + 1) * P)
+            nc.sync.dma_start(values[k][:], tab[0, block, :])
+            nc.sync.dma_start(streams[k][:], y[block, :])
+            nc.sync.dma_start(gates[k][:], tab[1, block, :])
+        block = slice(rows - P, rows)
+        nc.sync.dma_start(values[-1][:], tab[0, block, :])
+        nc.sync.dma_start(streams[-1][:, : entries - PIECE], y[block, : entries - PIECE])
+        nc.sync.dma_start(weights[:], w.rearrange("(k p) m -> p k m", p=P))
+        nc.sync.dma_start(gates[-1][:], tab[1, block, :])
+        nc.sync.dma_start(streams[-1][:, entries - PIECE :], y[block, entries - PIECE :])
 
         for k in range(blocks):
-            block = slice(k * P, (k + 1) * P)
-            gates = held.tile([P, places], F32, name=f"gates{k}")
-            nc.sync.dma_start(gates[:], tab[1, block, :])
-            values = held.tile([P, places], F32, name=f"values{k}")
-            nc.sync.dma_start(values[:], tab[0, block, :])
-            stream = held.tile([P, entries], F32, name=f"stream{k}")
-            nc.sync.dma_start(stream[:], y[block, :])
+            least = work.tile([P, entries], F32, name="least")
+            gate = work.tile([P, entries], F32, name="gate")
+            x = held.tile([P, entries], BF16, name=f"x{k}")
             for c in range(pieces):
                 piece = offsets[:, c * PIECE // GROUP : (c + 1) * PIECE // GROUP]
-                gate = work.tile([P, PIECE], F32, name="gate")
-                nc.scalar.activation(gate[:], gates[:].indirect(piece), ACT.Tanh)
-                least = work.tile([P, PIECE], F32, name="least")
-                nc.vector.tensor_tensor(least[:], values[:].indirect(piece), stream[:, c * PIECE : (c + 1) * PIECE], ALU.min)
-                x = work.tile([P, PIECE], BF16, name="x")
-                nc.vector.tensor_tensor(x[:], least[:], gate[:], ALU.mult)
-                nc.tensor.matmul(sums[c][:], weights[:, k, :], x[:], start=(k == 0), stop=(k == blocks - 1))
+                cols = slice(c * PIECE, (c + 1) * PIECE)
+                nc.vector.tensor_tensor(least[:, cols], values[k][:].indirect(piece), streams[k][:, cols], ALU.min)
+                nc.scalar.activation(gate[:, cols], gates[k][:].indirect(piece), ACT.Tanh)
+            for q in range(parts):
+                cols = slice(q * PART, (q + 1) * PART)
+                nc.vector.tensor_tensor(x[:, cols], least[:, cols], gate[:, cols], ALU.mult)
+                nc.tensor.matmul(sums[q][:], weights[:, k, :], x[:, cols], start=(k == 0), stop=(k == blocks - 1))
 
-        for c in range(pieces):
-            result = work.tile([P, PIECE], F32, name="result")
-            nc.scalar.activation(result[:], sums[c][:], ACT.Relu, bias=bias[:])
-            nc.sync.dma_start(out[:, c * PIECE : (c + 1) * PIECE], result[:])
+        for q in range(parts):
+            result = held.tile([P, PART], F32, name=f"result{q}")
+            if q < parts // 2:
+                nc.scalar.activation(result[:], sums[q][:], ACT.Relu, bias=bias[:])
+            else:
+                nc.vector.tensor_scalar(result[:], sums[q][:], bias[:], 0.0, ALU.add, ALU.max)
+            nc.sync.dma_start(out[:, q * PART : (q + 1) * PART], result[:])

@@ -32,12 +32,13 @@ def tile_lookup_vg_mintanh_relu_kernel(tc, tab, y, w, b, offs, out):
         sums = [psum.tile([P, PART], F32, name=f"sums{q}") for q in range(parts)]
 
         nc.scalar.dma_start(bias[:], b)
-        nc.sync.dma_start(offsets[:], offs)
         for k in range(blocks - 1):
             block = slice(k * P, (k + 1) * P)
             nc.sync.dma_start(values[k][:], tab[0, block, :])
+            if k == 0:
+                nc.sync.dma_start(offsets[:], offs)
             nc.sync.dma_start(streams[k][:], y[block, :])
-            nc.sync.dma_start(gates[k][:], tab[1, block, :])
+            nc.scalar.dma_start(gates[k][:], tab[1, block, :])
         block = slice(rows - P, rows)
         nc.sync.dma_start(values[-1][:], tab[0, block, :])
         nc.sync.dma_start(streams[-1][:, : entries - PIECE], y[block, : entries - PIECE])
@@ -61,7 +62,7 @@ def tile_lookup_vg_mintanh_relu_kernel(tc, tab, y, w, b, offs, out):
 
         for q in range(parts):
             result = held.tile([P, PART], F32, name=f"result{q}")
-            if q < parts // 2:
+            if q < parts - 1:
                 nc.scalar.activation(result[:], sums[q][:], ACT.Relu, bias=bias[:])
             else:
                 nc.vector.tensor_scalar(result[:], sums[q][:], bias[:], 0.0, ALU.add, ALU.max)

import concourse.mybir as mybir

P = 128
GROUP = 16
PIECE = 512
PART = 256

FLOPS = 2 * 512 * 128 * 1024

BF16, F32, U16 = mybir.dt.bfloat16, mybir.dt.float32, mybir.dt.uint16
ALU = mybir.AluOpType
ACT = mybir.ActivationFunctionType


def tile_lookup_vg_mintanh_relu_kernel(tc, tab, y, w, b, offs, out):
    nc = tc.nc
    rows, places = tab.shape[1], tab.shape[2]
    entries, features = y.shape[1], w.shape[1]
    blocks, pieces, parts = rows // P, entries // PIECE, entries // PART

    with (
        tc.tile_pool(name="held", bufs=1) as held,
        tc.tile_pool(name="work", bufs=2) as work,
        tc.psum_pool(name="psum", bufs=1) as psum,
    ):
        offsets = held.tile([P, entries // GROUP], U16, name="offsets")
        weights = held.tile([P, blocks, features], BF16, name="weights")
        bias = held.tile([P, 1], F32, name="bias")
        values = [held.tile([P, places], F32, name=f"values{k}") for k in range(blocks)]
        gates = [held.tile([P, places], F32, name=f"gates{k}") for k in range(blocks)]
        streams = [held.tile([P, entries], F32, name=f"stream{k}") for k in range(blocks)]
        sums = [psum.tile([P, PART], F32, name=f"sums{q}") for q in range(parts)]

        nc.scalar.dma_start(bias[:], b)
        for k in range(blocks - 1):
            block = slice(k * P, (k + 1) * P)
            nc.sync.dma_start(values[k][:], tab[0, block, :])
            if k == 0:
                nc.sync.dma_start(offsets[:], offs)
            nc.sync.dma_start(streams[k][:], y[block, :])
            nc.scalar.dma_start(gates[k][:], tab[1, block, :])
        block = slice(rows - P, rows)
        nc.sync.dma_start(values[-1][:], tab[0, block, :])
        nc.sync.dma_start(streams[-1][:, : entries - PIECE], y[block, : entries - PIECE])
        nc.sync.dma_start(weights[:], w.rearrange("(k p) m -> p k m", p=P))
        nc.sync.dma_start(gates[-1][:], tab[1, block, :])
        nc.sync.dma_start(streams[-1][:, entries - PIECE :], y[block, entries - PIECE :])

        for k in range(blocks):
            least = work.tile([P, entries], F32, name="least")
            gate = work.tile([P, entries], F32, name="gate")
            x = held.tile([P, entries], BF16, name=f"x{k}")
            for c in range(pieces):
                piece = offsets[:, c * PIECE // GROUP : (c + 1) * PIECE // GROUP]
                cols = slice(c * PIECE, (c + 1) * PIECE)
                nc.vector.tensor_tensor(least[:, cols], values[k][:].indirect(piece), streams[k][:, cols], ALU.min)
                nc.scalar.activation(gate[:, cols], gates[k][:].indirect(piece), ACT.Tanh)
            for q in range(parts):
                cols = slice(q * PART, (q + 1) * PART)
                nc.vector.tensor_tensor(x[:, cols], least[:, cols], gate[:, cols], ALU.mult)
                nc.tensor.matmul(sums[q][:], weights[:, k, :], x[:, cols], start=(k == 0), stop=(k == blocks - 1))

        for q in range(parts):
            result = held.tile([P, PART], F32, name=f"result{q}")
            if q < parts - 1:
                nc.scalar.activation(result[:], sums[q][:], ACT.Relu, bias=bias[:])
            else:
                nc.vector.tensor_scalar(result[:], sums[q][:], bias[:], 0.0, ALU.add, ALU.max)
            nc.sync.dma_start(out[:, q * PART : (q + 1) * PART], result[:])
